import numpy as np
import ml_dtypes


def mxq(x, axis, fmt="e4m3"):
    dtype, down = {"e4m3": (ml_dtypes.float8_e4m3fn, 7), "e5m2": (ml_dtypes.float8_e5m2, 14)}[fmt]
    v = np.moveaxis(np.asarray(x, np.float32).astype(ml_dtypes.bfloat16).astype(np.float64), axis, -1)
    blocks = v.reshape(v.shape[:-1] + (-1, 32))
    amax = np.abs(blocks).max(-1, keepdims=True)
    byte = np.maximum(np.where(amax > 0, np.frexp(amax)[1] - 1 + 127, 0) - down, 1)
    scale = np.exp2(byte - 127.0)
    codes = (blocks / scale).astype(np.float32).astype(dtype).astype(np.float64)
    return np.moveaxis((codes * scale).reshape(v.shape), -1, axis)


WIDE = False


def mx_kscale(k):
    if not WIDE:
        return np.ones(k)
    levels = np.array([24, -24, 12, -12, 0])
    if k % 512:
        return np.exp2(np.random.permutation(np.resize(levels, k // 32))).repeat(32)
    a = np.empty((k // 512, 16))
    for p in range(k // 512):
        a[p, :8] = np.random.permutation(np.resize(levels, 8))
        for g in range(8):
            far = levels[np.abs(levels - a[p, g]) >= 10]
            a[p, g + 8] = far[np.random.randint(len(far))]
    return np.exp2(a.ravel()).repeat(32)


def f64(x):
    return np.asarray(x).astype(np.float64)


def striped(idx):
    return np.tile(idx.reshape(-1, 16).T, (8, 1)).astype(np.uint16)


def unstriped(offs):
    return offs[:16].T.reshape(-1).astype(np.int64)


E2M1 = np.array([0.0, 0.5, 1.0, 1.5, 2.0, 3.0, 4.0, 6.0, -0.0, -0.5, -1.0, -1.5, -2.0, -3.0, -4.0, -6.0])


def pack_weight(w, fmt):
    k, n = w.shape
    w = f64(np.asarray(w, np.float32).astype(ml_dtypes.bfloat16)).reshape(k // 32, 32, n)
    amax = np.abs(w).max(1)
    if fmt == "e4m3":
        byte = np.frexp(amax)[1] - 1 + 127 - 7
    else:
        mant, ex = np.frexp(amax / 6.0)
        byte = np.where(mant > 0.5, ex, ex - 1) + 127
    byte = np.clip(np.where(amax > 0, byte, 1), 1, 254)
    scaled = (w * np.exp2(127.0 - byte)[:, None, :]).reshape(k, n).astype(np.float32)
    by_word = np.ascontiguousarray(scaled.reshape(k // 512, 128, 4, n).transpose(0, 1, 3, 2))
    if fmt == "e4m3":
        words = by_word.astype(ml_dtypes.float8_e4m3fn).view(np.uint8)
    else:
        c = by_word.astype(ml_dtypes.float4_e2m1fn).view(np.uint8) & 0xF
        words = (c[..., 0::2] | (c[..., 1::2] << 4)).reshape(k // 512, 128, 2 * n)
    return np.ascontiguousarray(words), np.ascontiguousarray(byte.astype(np.uint8).reshape(k // 512, 16, n))


def unpack_weight(words, scales, fmt):
    g, _, n = scales.shape
    words = np.ascontiguousarray(words).reshape(g, 128, n, -1)
    if fmt == "e4m3":
        vals = words.view(ml_dtypes.float8_e4m3fn).astype(np.float64)
    else:
        nib = np.empty((g, 128, n, 4), np.uint8)
        nib[..., 0::2] = words & 0xF
        nib[..., 1::2] = words >> 4
        vals = E2M1[nib]
    vals = vals * np.repeat(np.exp2(scales.astype(np.float64) - 127.0), 8, axis=1)[..., None]
    return vals.transpose(0, 1, 3, 2).reshape(g * 512, n)


def sigm(f):
    return 1.0 / (1.0 + np.exp(-np.maximum(f, -700.0)))


K, M, N, T, J = 512, 512, 512, 2048, 1024


def setup_inputs():
    n = np.random.standard_normal
    s = mx_kscale(K)[:, None]
    s2 = mx_kscale(M)[:, None]
    h = np.tanh(n((N, T)))
    p_tab = pack_weight(h * s2, "e4m3")
    p_wz = pack_weight(n((K, N)) / np.sqrt(K) / s, "e2m1")
    p_wr = pack_weight(n((K, N)) / np.sqrt(K) / s, "e2m1")
    p_wn = pack_weight(n((K, N)) / np.sqrt(K) / s, "e2m1")
    return {
        "x": (n((K, J)) * s).astype(np.float32),
        "tab_words": p_tab[0],
        "tab_scales": p_tab[1],
        "wz_words": p_wz[0],
        "wz_scales": p_wz[1],
        "uz": (n((M, N)) / np.sqrt(M) / s2).astype(np.float32),
        "wr_words": p_wr[0],
        "wr_scales": p_wr[1],
        "ur": (n((M, N)) / np.sqrt(M) / s2).astype(np.float32),
        "wn_words": p_wn[0],
        "wn_scales": p_wn[1],
        "un": (n((M, N)) / np.sqrt(M) / s2).astype(np.float32),
        "bz": (0.3 * n(N)).astype(np.float32),
        "br": (0.3 * n(N)).astype(np.float32),
        "bn": (0.3 * n(N)).astype(np.float32),
        "hT": (h).astype(np.float32),
        "wgo": np.tile(np.random.uniform(0.5, 2.0, J), (128, 1)).astype(np.float32),
        "offs": striped(np.random.permutation(T)[:J]),
    }


def reference(x, tab_words, tab_scales, wz_words, wz_scales, uz, wr_words, wr_scales, ur, wn_words, wn_scales, un, bz, br, bn, hT, wgo, offs):
    idx = unstriped(offs)
    x_ = mxq(f64(x), 0, "e4m3")
    tab_ = unpack_weight(tab_words, tab_scales, "e4m3")[:, idx]
    wz_ = unpack_weight(wz_words, wz_scales, "e2m1")
    uz_ = mxq(f64(uz), 0, "e4m3")
    wr_ = unpack_weight(wr_words, wr_scales, "e2m1")
    ur_ = mxq(f64(ur), 0, "e4m3")
    wn_ = unpack_weight(wn_words, wn_scales, "e2m1")
    un_ = mxq(f64(un), 0, "e4m3")
    sz = wz_.T @ x_ + uz_.T @ tab_
    z = sigm(sz + f64(bz)[:, None])
    sr = wr_.T @ x_ + ur_.T @ tab_
    r = sigm(sr + f64(br)[:, None])
    xn = wn_.T @ x_
    hn = un_.T @ tab_
    cd = np.tanh(xn + f64(bn)[:, None] + r * hn)
    out = np.zeros((N, T))
    out[:, idx] = f64(wgo)[0] * (f64(hT)[:, idx] + z * (cd - f64(hT)[:, idx]))
    return out

@@ -1,0 +1,206 @@
+from contextlib import ExitStack
+
+import concourse.mybir as mybir
+
+K, M, N, T, J = 512, 512, 512, 2048, 1024
+FLOPS = 6 * 2 * K * N * J
+
+F32 = mybir.dt.float32
+BF16 = mybir.dt.bfloat16
+I32 = mybir.dt.int32
+U32 = mybir.dt.uint32
+U16 = mybir.dt.uint16
+U8 = mybir.dt.uint8
+FP8X4 = mybir.dt.float8_e4m3fn_x4
+FP4X4 = mybir.dt.float4_e2m1fn_x4
+ACT = mybir.ActivationFunctionType
+ALU = mybir.AluOpType
+
+P = 128
+PACK = 4
+JC = 512
+HALVES = J // JC
+TILES = N // P
+LIST_COLS = JC // 16
+VECTOR_STEPS = (0,)
+
+
+def tile_list_tgn_gru_kernel(
+    tc, x, tab_words, tab_scales, wz_words, wz_scales, uz, wr_words, wr_scales, ur,
+    wn_words, wn_scales, un, bz, br, bn, hT, wgo, offs, out,
+):
+    nc = tc.nc
+    gates = ("r", "n", "z")
+    w_words = {"r": wr_words, "n": wn_words, "z": wz_words}
+    w_scales = {"r": wr_scales, "n": wn_scales, "z": wz_scales}
+    u_dram = {"r": ur, "n": un, "z": uz}
+    b_dram = {"r": br, "n": bn, "z": bz}
+
+    with ExitStack() as ctx:
+        keep = ctx.enter_context(tc.tile_pool(name="keep", bufs=1))
+        work = ctx.enter_context(tc.tile_pool(name="work", bufs=3))
+        psum = ctx.enter_context(tc.psum_pool(name="psum", bufs=2))
+
+        offsets = keep.tile([P, J // 16], U16, name="offsets")
+        nc.sync.dma_start(offsets[:], offs)
+
+        def picks(half):
+            return offsets[:, half * LIST_COLS:(half + 1) * LIST_COLS]
+
+        tab_plane = keep.tile([P, T], U8, name="tab_plane", align_bytes=64)
+        nc.vector.memset(tab_plane[:].bitcast(I32), 0)
+        w_plane = keep.tile([P, len(gates) * N], U8, name="w_plane", align_bytes=64)
+        nc.gpsimd.memset(w_plane[:].bitcast(I32), 0)
+        warm = keep.tile([P, 2], F32, name="warm")
+        nc.vector.memset(warm[:, 0:1], 0.0)
+        nc.scalar.activation(warm[:, 1:2], warm[:, 0:1], ACT.Sigmoid)
+
+        tab = keep.tile([P, T], I32, name="tab", align_bytes=64)
+        for q in range(4):
+            nc.sync.dma_start(tab_plane[32 * q:32 * q + 4, :].bitcast(I32),
+                              tab_scales[0, 4 * q:4 * q + 4, :].bitcast(I32))
+        nc.sync.dma_start(tab[:], tab_words[0].rearrange("p t i -> p (t i)").bitcast(I32))
+        for gi, g in enumerate(gates):
+            nc.gpsimd.dma_start(w_plane[0:16, gi * N:(gi + 1) * N].bitcast(I32), w_scales[g][0].bitcast(I32))
+        for q in range(1, 4):
+            nc.scalar.dma_start(w_plane[32 * q:32 * q + 4, :].bitcast(I32), w_plane[4 * q:4 * q + 4, :].bitcast(I32))
+
+        x_raw = [keep.tile([P, PACK, JC], F32, name=f"x_raw{h}") for h in range(HALVES)]
+
+        def load_x(h):
+            nc.sync.dma_start(x_raw[h][:], x[:, h * JC:(h + 1) * JC].rearrange("(p i) j -> p i j", i=PACK))
+
+        load_x(0)
+        w_codes = {}
+        u_first = {}
+        u_rest = {}
+        bias = {}
+        for g in gates:
+            w_codes[g] = keep.tile([P, 2 * N], U8, name=f"w_codes_{g}", align_bytes=64)
+            u_first[g] = keep.tile([P, PACK, P], F32, name=f"u_first_{g}")
+            u_rest[g] = keep.tile([P, PACK, N - P], F32, name=f"u_rest_{g}")
+            bias[g] = keep.tile([P, TILES], F32, name=f"bias_{g}")
+            nc.sync.dma_start(u_first[g][:], u_dram[g][:, 0:P].rearrange("(p i) n -> p i n", i=PACK))
+            nc.sync.dma_start(w_codes[g][:].bitcast(I32), w_words[g][0].bitcast(I32))
+        with nc.allow_non_contiguous_dma(reason="a bias is one value a partition"):
+            for g in gates:
+                nc.gpsimd.dma_start(bias[g][:], b_dram[g].rearrange("(t p) -> p t", p=P))
+        state = [keep.tile([P, T], F32, name=f"state{t}") for t in range(TILES)]
+        load_x(1)
+        nc.sync.dma_start(state[0][:], hT[0:P, :])
+        weight = [keep.tile([P, JC], F32, name=f"weight{h}") for h in range(HALVES)]
+        for h in range(HALVES):
+            nc.sync.dma_start(weight[h][:], wgo[:, h * JC:(h + 1) * JC])
+        for g in gates:
+            nc.sync.dma_start(u_rest[g][:], u_dram[g][:, P:N].rearrange("(p i) n -> p i n", i=PACK))
+        for t in range(1, TILES):
+            nc.sync.dma_start(state[t][:], hT[t * P:(t + 1) * P, :])
+
+        pages = [keep.tile([P, T], F32, name=f"page{b}") for b in range(2)]
+        nc.vector.memset(pages[0][:], 0.0)
+        nc.gpsimd.memset(pages[1][:], 0.0)
+
+        def quantise(raw, width, name):
+            grouped = keep.tile([P, width, PACK], BF16, name=f"{name}_grouped", align_bytes=64)
+            nc.scalar.copy(grouped[:].rearrange("p (c s) i -> p c i s", s=4),
+                           raw.rearrange("p i (c s) -> p c i s", s=4))
+            codes = keep.tile([P, width], U32, name=f"{name}_codes", align_bytes=64)
+            plane = keep.tile([P, width], U8, name=f"{name}_plane", align_bytes=64)
+            nc.vector.quantize_mx(out=codes[:].bitcast(FP8X4), scales=plane[:],
+                                  in_=grouped[:].rearrange("p w i -> p (w i)"))
+            return codes, plane
+
+        v_op = {}
+        x_op = {}
+        u_op = {}
+
+        def gather_table(h):
+            plane = keep.tile([P, JC], U8, name=f"v_plane{h}", align_bytes=64)
+            nc.vector.tensor_copy(plane[:], tab_plane[:].indirect(picks(h)))
+            codes = keep.tile([P, JC], U32, name=f"v_codes{h}", align_bytes=64)
+            nc.vector.tensor_copy(codes[:], tab[:].bitcast(U32).indirect(picks(h)))
+            v_op[h] = (codes, plane)
+
+        def quantise_u(t):
+            for g in gates:
+                raw = u_first[g][:] if t == 0 else u_rest[g][:, :, (t - 1) * P:t * P]
+                u_op[g, t] = quantise(raw, P, f"u_{g}{t}")
+
+        def w_pass(acc, g, t, h, start, stop):
+            gi = gates.index(g)
+            nc.tensor.matmul_mx(
+                out=acc[:], lhsT=w_codes[g][:, 2 * P * t:2 * P * (t + 1)].bitcast(FP4X4),
+                lhsT_scale=w_plane[:, gi * N + t * P:gi * N + (t + 1) * P],
+                rhs=x_op[h][0][:].bitcast(FP8X4), rhs_scale=x_op[h][1][:], start=start, stop=stop)
+
+        def u_pass(acc, g, t, h, start, stop):
+            nc.tensor.matmul_mx(
+                out=acc[:], lhsT=u_op[g, t][0][:].bitcast(FP8X4), lhsT_scale=u_op[g, t][1][:],
+                rhs=v_op[h][0][:].bitcast(FP8X4), rhs_scale=v_op[h][1][:], start=start, stop=stop)
+
+        def gates_and_candidate(t, h):
+            sr = psum.tile([P, JC], F32, name="sr")
+            hn = psum.tile([P, JC], F32, name="hn")
+            xn = psum.tile([P, JC], F32, name="xn")
+            sz = psum.tile([P, JC], F32, name="sz")
+            w_pass(sr, "r", t, h, True, False)
+            u_pass(sr, "r", t, h, False, True)
+            u_pass(hn, "n", t, h, True, True)
+            w_pass(xn, "n", t, h, True, True)
+            w_pass(sz, "z", t, h, True, False)
+            u_pass(sz, "z", t, h, False, True)
+            r = work.tile([P, JC], F32, name="r")
+            nc.scalar.activation(r[:], sr[:], ACT.Sigmoid, bias=bias["r"][:, t:t + 1])
+            z = work.tile([P, JC], F32, name="z")
+            nc.scalar.activation(z[:], sz[:], ACT.Sigmoid, bias=bias["z"][:, t:t + 1])
+            rh = work.tile([P, JC], F32, name="rh")
+            nc.vector.tensor_tensor(rh[:], hn[:], r[:], ALU.mult)
+            pre = work.tile([P, JC], F32, name="pre")
+            nc.vector.tensor_tensor(pre[:], xn[:], rh[:], ALU.add)
+            cd = work.tile([P, JC], F32, name="cd")
+            nc.scalar.activation(cd[:], pre[:], ACT.Tanh, bias=bias["n"][:, t:t + 1])
+            return z, cd
+
+        def blend(t, h, z, cd, on_vector):
+            eng = nc.vector if on_vector else nc.gpsimd
+            old = work.tile([P, JC], F32, name="old")
+            nc.vector.tensor_copy(old[:], state[t][:].indirect(picks(h)))
+            diff = work.tile([P, JC], F32, name="diff")
+            eng.tensor_tensor(diff[:], cd[:], old[:], ALU.subtract)
+            step = work.tile([P, JC], F32, name="step")
+            eng.tensor_tensor(step[:], z[:], diff[:], ALU.mult)
+            new = work.tile([P, JC], F32, name="new")
+            eng.tensor_tensor(new[:], old[:], step[:], ALU.add)
+            if on_vector:
+                return new
+            weighted = work.tile([P, JC], F32, name="weighted")
+            eng.tensor_tensor(weighted[:], new[:], weight[h][:], ALU.mult)
+            return weighted
+
+        def place(t, h, values, on_vector):
+            page = pages[t % 2]
+            if on_vector:
+                nc.vector.tensor_tensor(page[:].indirect(picks(h)), values[:], weight[h][:], ALU.mult)
+            else:
+                nc.vector.tensor_copy(page[:].indirect(picks(h)), values[:])
+            if h == HALVES - 1:
+                nc.sync.dma_start(out[t * P:(t + 1) * P, :], page[:])
+
+        gather_table(0)
+        x_op[0] = quantise(x_raw[0][:], JC, "x0")
+        quantise_u(0)
+        gather_table(1)
+        steps = [(t, h) for t in range(TILES) for h in range(HALVES)]
+        waiting = None
+        for s, (t, h) in enumerate(steps):
+            on_vector = s in VECTOR_STEPS
+            z, cd = gates_and_candidate(t, h)
+            if s == 0:
+                x_op[1] = quantise(x_raw[1][:], JC, "x1")
+            if h == 0 and t + 1 < TILES:
+                quantise_u(t + 1)
+            values = blend(t, h, z, cd, on_vector)
+            if waiting is not None:
+                place(*waiting)
+            waiting = (t, h, values, on_vector)
+        place(*waiting)

@@ -1,6 +1,7 @@
 from contextlib import ExitStack
 
 import concourse.mybir as mybir
+from concourse.masks import make_identity
 
 K, M, N, T, J = 512, 512, 512, 2048, 1024
 FLOPS = 6 * 2 * K * N * J
@@ -21,8 +22,9 @@ PACK = 4
 JC = 512
 HALVES = J // JC
 TILES = N // P
+BLOCKS = JC // P
 LIST_COLS = JC // 16
-VECTOR_STEPS = (0,)
+LAG = 0
 
 
 def tile_list_tgn_gru_kernel(
@@ -38,8 +40,8 @@ def tile_list_tgn_gru_kernel(
 
     with ExitStack() as ctx:
         keep = ctx.enter_context(tc.tile_pool(name="keep", bufs=1))
-        work = ctx.enter_context(tc.tile_pool(name="work", bufs=3))
-        psum = ctx.enter_context(tc.psum_pool(name="psum", bufs=2))
+        work = ctx.enter_context(tc.tile_pool(name="work", bufs=2))
+        psum = ctx.enter_context(tc.psum_pool(name="psum", bufs=1))
 
         offsets = keep.tile([P, J // 16], U16, name="offsets")
         nc.sync.dma_start(offsets[:], offs)
@@ -50,60 +52,81 @@ def tile_list_tgn_gru_kernel(
         tab_plane = keep.tile([P, T], U8, name="tab_plane", align_bytes=64)
         nc.vector.memset(tab_plane[:].bitcast(I32), 0)
         w_plane = keep.tile([P, len(gates) * N], U8, name="w_plane", align_bytes=64)
-        nc.gpsimd.memset(w_plane[:].bitcast(I32), 0)
-        warm = keep.tile([P, 2], F32, name="warm")
-        nc.vector.memset(warm[:, 0:1], 0.0)
-        nc.scalar.activation(warm[:, 1:2], warm[:, 0:1], ACT.Sigmoid)
+        nc.vector.memset(w_plane[:].bitcast(I32), 0)
 
+        rows = keep.tile([P, P], F32, name="rows")
+        nc.gpsimd.memset(rows[:], 0.0)
+        ident = keep.tile([P, P], F32, name="ident")
+        make_identity(nc, ident[:])
+        w_rows = keep.tile([16, len(gates) * N], U8, name="w_rows")
+        for gi, g in enumerate(gates):
+            nc.sync.dma_start(w_rows[:, gi * N:(gi + 1) * N].bitcast(I32), w_scales[g][0].bitcast(I32))
         tab = keep.tile([P, T], I32, name="tab", align_bytes=64)
         for q in range(4):
             nc.sync.dma_start(tab_plane[32 * q:32 * q + 4, :].bitcast(I32),
                               tab_scales[0, 4 * q:4 * q + 4, :].bitcast(I32))
         nc.sync.dma_start(tab[:], tab_words[0].rearrange("p t i -> p (t i)").bitcast(I32))
+        n_w = J // P
+
         for gi, g in enumerate(gates):
-            nc.gpsimd.dma_start(w_plane[0:16, gi * N:(gi + 1) * N].bitcast(I32), w_scales[g][0].bitcast(I32))
-        for q in range(1, 4):
-            nc.scalar.dma_start(w_plane[32 * q:32 * q + 4, :].bitcast(I32), w_plane[4 * q:4 * q + 4, :].bitcast(I32))
+            nc.gpsimd.dma_start(rows[n_w + gi * TILES:n_w + (gi + 1) * TILES, :],
+                                b_dram[g].rearrange("(t p) -> t p", p=P))
+        nc.gpsimd.dma_start(rows[0:n_w, :], wgo[0].rearrange("(c p) -> c p", p=P))
 
-        x_raw = [keep.tile([P, PACK, JC], F32, name=f"x_raw{h}") for h in range(HALVES)]
+        x_raw = {}
 
-        def load_x(h):
+        def load_x(h, tag):
+            x_raw[h] = keep.tile([P, PACK, JC], F32, name=f"x_raw{h}", tag=tag, align_bytes=64)
             nc.sync.dma_start(x_raw[h][:], x[:, h * JC:(h + 1) * JC].rearrange("(p i) j -> p i j", i=PACK))
 
-        load_x(0)
+        load_x(0, "x_raw0")
         w_codes = {}
         u_first = {}
         u_rest = {}
-        bias = {}
         for g in gates:
             w_codes[g] = keep.tile([P, 2 * N], U8, name=f"w_codes_{g}", align_bytes=64)
-            u_first[g] = keep.tile([P, PACK, P], F32, name=f"u_first_{g}")
-            u_rest[g] = keep.tile([P, PACK, N - P], F32, name=f"u_rest_{g}")
-            bias[g] = keep.tile([P, TILES], F32, name=f"bias_{g}")
+            u_first[g] = keep.tile([P, PACK, P], F32, name=f"u_first_{g}", align_bytes=64)
             nc.sync.dma_start(u_first[g][:], u_dram[g][:, 0:P].rearrange("(p i) n -> p i n", i=PACK))
             nc.sync.dma_start(w_codes[g][:].bitcast(I32), w_words[g][0].bitcast(I32))
-        with nc.allow_non_contiguous_dma(reason="a bias is one value a partition"):
-            for g in gates:
-                nc.gpsimd.dma_start(bias[g][:], b_dram[g].rearrange("(t p) -> p t", p=P))
-        state = [keep.tile([P, T], F32, name=f"state{t}") for t in range(TILES)]
-        load_x(1)
-        nc.sync.dma_start(state[0][:], hT[0:P, :])
-        weight = [keep.tile([P, JC], F32, name=f"weight{h}") for h in range(HALVES)]
-        for h in range(HALVES):
-            nc.sync.dma_start(weight[h][:], wgo[:, h * JC:(h + 1) * JC])
-        for g in gates:
-            nc.sync.dma_start(u_rest[g][:], u_dram[g][:, P:N].rearrange("(p i) n -> p i n", i=PACK))
-        for t in range(1, TILES):
+        for q in range(4):
+            nc.sync.dma_start(w_plane[32 * q:32 * q + 4, :].bitcast(I32), w_rows[4 * q:4 * q + 4, :].bitcast(I32))
+        state = {}
+
+        def load_state(t, tag):
+            state[t] = keep.tile([P, T], F32, name=f"state{t}", tag=tag, align_bytes=64)
             nc.sync.dma_start(state[t][:], hT[t * P:(t + 1) * P, :])
 
-        pages = [keep.tile([P, T], F32, name=f"page{b}") for b in range(2)]
-        nc.vector.memset(pages[0][:], 0.0)
-        nc.gpsimd.memset(pages[1][:], 0.0)
+        def load_u(g, t0, t1, tag):
+            raw = keep.tile([P, PACK, (t1 - t0) * P], F32, name=f"u_raw_{g}{t0}", tag=tag, align_bytes=64)
+            nc.sync.dma_start(raw[:], u_dram[g][:, t0 * P:t1 * P].rearrange("(p i) n -> p i n", i=PACK))
+            for t in range(t0, t1):
+                u_rest[g, t] = raw[:, :, (t - t0) * P:(t - t0 + 1) * P]
 
-        def quantise(raw, width, name):
-            grouped = keep.tile([P, width, PACK], BF16, name=f"{name}_grouped", align_bytes=64)
-            nc.scalar.copy(grouped[:].rearrange("p (c s) i -> p c i s", s=4),
-                           raw.rearrange("p i (c s) -> p c i s", s=4))
+        pages = []
+
+        def clear_page(tag, eng):
+            page = keep.tile([P, T], F32, name=f"page{len(pages)}", tag=tag, align_bytes=64)
+            eng.memset(page[:], 0.0)
+            pages.append(page)
+
+        clear_page("page0", nc.vector)
+
+        n_cols = n_w + len(gates) * TILES
+        turned = psum.tile([P, P], F32, name="keep_n", tag="keep_n")
+        nc.tensor.transpose(turned[:], rows[:], ident[:])
+        cols = keep.tile([P, n_cols], F32, name="cols")
+        nc.scalar.copy(cols[:], turned[:, 0:n_cols])
+        minus_w = keep.tile([P, n_w], F32, name="minus_w")
+        nc.vector.tensor_scalar(minus_w[:], cols[:, 0:n_w], -1.0, None, ALU.mult)
+
+        def bias(g, t):
+            c = n_w + gates.index(g) * TILES + t
+            return cols[:, c:c + 1]
+
+        def quantise(raw, width, name, copy, tag):
+            grouped = keep.tile([P, width, PACK], BF16, name=f"{name}_grouped", tag=tag, align_bytes=64)
+            copy(grouped[:].rearrange("p (c s) i -> p c i s", s=4),
+                 raw.rearrange("p i (c s) -> p c i s", s=4))
             codes = keep.tile([P, width], U32, name=f"{name}_codes", align_bytes=64)
             plane = keep.tile([P, width], U8, name=f"{name}_plane", align_bytes=64)
             nc.vector.quantize_mx(out=codes[:].bitcast(FP8X4), scales=plane[:],
@@ -114,8 +137,8 @@ def tile_list_tgn_gru_kernel(
         x_op = {}
         u_op = {}
 
-        def gather_table(h):
-            plane = keep.tile([P, JC], U8, name=f"v_plane{h}", align_bytes=64)
+        def gather_table(h, tag):
+            plane = keep.tile([P, JC], U8, name=f"v_plane{h}", tag=tag, align_bytes=64)
             nc.vector.tensor_copy(plane[:], tab_plane[:].indirect(picks(h)))
             codes = keep.tile([P, JC], U32, name=f"v_codes{h}", align_bytes=64)
             nc.vector.tensor_copy(codes[:], tab[:].bitcast(U32).indirect(picks(h)))
@@ -123,8 +146,9 @@ def tile_list_tgn_gru_kernel(
 
         def quantise_u(t):
             for g in gates:
-                raw = u_first[g][:] if t == 0 else u_rest[g][:, :, (t - 1) * P:t * P]
-                u_op[g, t] = quantise(raw, P, f"u_{g}{t}")
+                raw = u_first[g][:] if t == 0 else u_rest[g, t]
+                u_op[g, t] = quantise(raw, P, f"u_{g}{t}", nc.vector.tensor_copy if t == 0 else nc.scalar.copy,
+                                      f"u_{g}{t}_grouped")
 
         def w_pass(acc, g, t, h, start, stop):
             gi = gates.index(g)
@@ -138,7 +162,29 @@ def tile_list_tgn_gru_kernel(
                 out=acc[:], lhsT=u_op[g, t][0][:].bitcast(FP8X4), lhsT_scale=u_op[g, t][1][:],
                 rhs=v_op[h][0][:].bitcast(FP8X4), rhs_scale=v_op[h][1][:], start=start, stop=stop)
 
-        def gates_and_candidate(t, h):
+        def block(b):
+            return slice(b * P, (b + 1) * P)
+
+        def turn(name, *terms):
+            bank = psum.tile([P, JC], F32, name=name, tag=name)
+            for b in range(BLOCKS):
+                for i, term in enumerate(terms):
+                    nc.tensor.matmul(bank[:, block(b)], lhsT=term[:, block(b)], rhs=ident[:], is_transpose=True,
+                                     start=(i == 0), stop=(i == len(terms) - 1))
+            return bank
+
+        steps = [(t, h) for t in range(TILES) for h in range(HALVES)]
+        mix = [keep.tile([P, JC], F32, name=f"mix{b}") for b in range(2)]
+        mix2 = [keep.tile([P, JC], F32, name=f"mixb{b}") for b in range(2)]
+        first_rh = [keep.tile([P, JC], F32, name=f"first_rh{b}") for b in range(2)]
+        z_of = {}
+        xn_of = {}
+        rh_of = {}
+        keep_of = {}
+        fresh_of = {}
+
+        def products(s):
+            t, h = steps[s]
             sr = psum.tile([P, JC], F32, name="sr")
             hn = psum.tile([P, JC], F32, name="hn")
             xn = psum.tile([P, JC], F32, name="xn")
@@ -149,58 +195,103 @@ def tile_list_tgn_gru_kernel(
             w_pass(xn, "n", t, h, True, True)
             w_pass(sz, "z", t, h, True, False)
             u_pass(sz, "z", t, h, False, True)
-            r = work.tile([P, JC], F32, name="r")
-            nc.scalar.activation(r[:], sr[:], ACT.Sigmoid, bias=bias["r"][:, t:t + 1])
-            z = work.tile([P, JC], F32, name="z")
-            nc.scalar.activation(z[:], sz[:], ACT.Sigmoid, bias=bias["z"][:, t:t + 1])
-            rh = work.tile([P, JC], F32, name="rh")
-            nc.vector.tensor_tensor(rh[:], hn[:], r[:], ALU.mult)
-            pre = work.tile([P, JC], F32, name="pre")
-            nc.vector.tensor_tensor(pre[:], xn[:], rh[:], ALU.add)
-            cd = work.tile([P, JC], F32, name="cd")
-            nc.scalar.activation(cd[:], pre[:], ACT.Tanh, bias=bias["n"][:, t:t + 1])
-            return z, cd
-
-        def blend(t, h, z, cd, on_vector):
-            eng = nc.vector if on_vector else nc.gpsimd
-            old = work.tile([P, JC], F32, name="old")
-            nc.vector.tensor_copy(old[:], state[t][:].indirect(picks(h)))
-            diff = work.tile([P, JC], F32, name="diff")
-            eng.tensor_tensor(diff[:], cd[:], old[:], ALU.subtract)
-            step = work.tile([P, JC], F32, name="step")
-            eng.tensor_tensor(step[:], z[:], diff[:], ALU.mult)
-            new = work.tile([P, JC], F32, name="new")
-            eng.tensor_tensor(new[:], old[:], step[:], ALU.add)
-            if on_vector:
-                return new
-            weighted = work.tile([P, JC], F32, name="weighted")
-            eng.tensor_tensor(weighted[:], new[:], weight[h][:], ALU.mult)
-            return weighted
-
-        def place(t, h, values, on_vector):
-            page = pages[t % 2]
-            if on_vector:
-                nc.vector.tensor_tensor(page[:].indirect(picks(h)), values[:], weight[h][:], ALU.mult)
+            if s == 1:
+                r = keep.tile([P, JC], F32, name="second_r", align_bytes=64)
             else:
-                nc.vector.tensor_copy(page[:].indirect(picks(h)), values[:])
+                r = work.tile([P, JC], F32, name="r")
+            nc.scalar.activation(r[:], sr[:], ACT.Sigmoid, bias=bias("r", t))
+            if s == 0:
+                xb = xn
+            else:
+                xb = work.tile([P, JC], F32, name="xb")
+                nc.scalar.activation(xb[:], xn[:], ACT.Identity, bias=bias("n", t))
+            z = work.tile([P, JC], F32, name="z")
+            nc.scalar.activation(z[:], sz[:], ACT.Sigmoid, bias=bias("z", t))
+            rh = first_rh[s] if s < 2 else mix2[(s - 1) % 2]
+            nc.vector.tensor_tensor(rh[:], hn[:], r[:], ALU.mult)
+            z_of[s], xn_of[s], rh_of[s] = z, xb, rh
+
+        def factors(s):
+            t, h = steps[s]
+            pre_t = turn("pre_t", xn_of[s], rh_of[s])
+            z_t = turn("z_t", z_of[s])
+            minus_cd_t = mix[s % 2]
+            nc.scalar.activation(minus_cd_t[:], pre_t[:], ACT.Tanh, scale=-1.0)
+            keep_t = work.tile([P, JC], F32, name="keep_t")
+            for b in range(BLOCKS):
+                c = h * BLOCKS + b
+                nc.scalar.activation(keep_t[:, block(b)], z_t[:, block(b)], ACT.Identity,
+                                     scale=minus_w[:, c:c + 1], bias=cols[:, c:c + 1])
+            keep_n = turn("keep_n", keep_t)
+            keep_sb = mix2[s % 2]
+            nc.scalar.copy(keep_sb[:], keep_n[:])
+            fresh_t = work.tile([P, JC], F32, name="fresh_t")
+            for b in range(BLOCKS):
+                c = h * BLOCKS + b
+                nc.vector.scalar_tensor_tensor(fresh_t[:, block(b)], keep_t[:, block(b)], cols[:, c:c + 1],
+                                               minus_cd_t[:, block(b)], ALU.subtract, ALU.mult)
+            fresh_n = turn("fresh_n", fresh_t)
+            fresh_sb = work.tile([P, JC], F32, name="fresh_sb", bufs=3)
+            nc.scalar.copy(fresh_sb[:], fresh_n[:])
+            keep_of[s], fresh_of[s] = keep_sb, fresh_sb
+
+        def first_candidate():
+            pre = keep.tile([P, JC], F32, name="first_pre")
+            nc.vector.tensor_tensor(pre[:], xn_of[0][:], rh_of[0][:], ALU.add)
+            cd = keep.tile([P, JC], F32, name="first_cd")
+            nc.scalar.activation(cd[:], pre[:], ACT.Tanh, bias=bias("n", 0))
+            return cd
+
+        def first_place(cd):
+            diff = keep.tile([P, JC], F32, name="first_diff")
+            nc.vector.tensor_tensor(diff[:], state[0][:].indirect(picks(0)), cd[:], ALU.subtract)
+            step = keep.tile([P, JC], F32, name="first_step")
+            nc.vector.scalar_tensor_tensor(step[:], z_of[0][:], 1.0, diff[:], ALU.subtract, ALU.mult)
+            new = keep.tile([P, JC], F32, name="first_new", tag="second_r", align_bytes=64)
+            nc.vector.tensor_tensor(new[:], cd[:], step[:], ALU.subtract)
+            nc.vector.tensor_tensor(pages[0][:].indirect(picks(0)), new[:], first_w[:], ALU.mult)
+
+        def look_up(s):
+            t, h = steps[s]
+            nc.vector.tensor_tensor(mix[s % 2][:], state[t][:].indirect(picks(h)), keep_of[s][:], ALU.mult)
+
+        def place(s):
+            t, h = steps[s]
+            kept = mix[s % 2]
+            page = pages[t % 2]
+            nc.vector.tensor_tensor(page[:].indirect(picks(h)), kept[:], fresh_of[s][:], ALU.add)
             if h == HALVES - 1:
+                if t + 2 < TILES:
+                    load_state(t + 2, "x_raw0" if t % 2 == 0 else "tab")
                 nc.sync.dma_start(out[t * P:(t + 1) * P, :], page[:])
 
-        gather_table(0)
-        x_op[0] = quantise(x_raw[0][:], JC, "x0")
+        gather_table(0, "v_plane0")
+        x_op[0] = quantise(x_raw[0][:], JC, "x0", nc.scalar.copy, "x0_grouped")
         quantise_u(0)
-        gather_table(1)
-        steps = [(t, h) for t in range(TILES) for h in range(HALVES)]
-        waiting = None
-        for s, (t, h) in enumerate(steps):
-            on_vector = s in VECTOR_STEPS
-            z, cd = gates_and_candidate(t, h)
-            if s == 0:
-                x_op[1] = quantise(x_raw[1][:], JC, "x1")
-            if h == 0 and t + 1 < TILES:
+        gather_table(1, "u_n0_grouped")
+        load_x(1, "tab")
+        u_tags = {"r": "u_first_r", "n": "u_first_n", "z": "u_r0_grouped"}
+        for g in gates:
+            load_u(g, 1, 2, u_tags[g])
+        load_state(0, "x_raw0")
+        first_w = keep.tile([P, JC], F32, name="first_w", tag="x0_grouped", align_bytes=64)
+        nc.sync.dma_start(first_w[:], wgo[:, 0:JC])
+        products(0)
+        x_op[1] = quantise(x_raw[1][:], JC, "x1", nc.vector.tensor_copy, "x1_grouped")
+        load_state(1, "tab")
+        cd = first_candidate()
+        products(1)
+        quantise_u(1)
+        clear_page("u_z1_grouped", nc.gpsimd)
+        for g in gates:
+            load_u(g, 2, TILES, u_tags[g])
+        first_place(cd)
+        for s in range(1, len(steps)):
+            t, h = steps[s]
+            factors(s)
+            look_up(s)
+            if h == 1 and 1 <= t < TILES - 1:
                 quantise_u(t + 1)
-            values = blend(t, h, z, cd, on_vector)
-            if waiting is not None:
-                place(*waiting)
-            waiting = (t, h, values, on_vector)
-        place(*waiting)
+            if s + 1 < len(steps):
+                products(s + 1)
+            place(s)

@@ -24,7 +24,6 @@ HALVES = J // JC
 TILES = N // P
 BLOCKS = JC // P
 LIST_COLS = JC // 16
-LAG = 0
 
 
 def tile_list_tgn_gru_kernel(
@@ -50,7 +49,7 @@ def tile_list_tgn_gru_kernel(
             return offsets[:, half * LIST_COLS:(half + 1) * LIST_COLS]
 
         tab_plane = keep.tile([P, T], U8, name="tab_plane", align_bytes=64)
-        nc.vector.memset(tab_plane[:].bitcast(I32), 0)
+        nc.gpsimd.memset(tab_plane[:].bitcast(I32), 0)
         w_plane = keep.tile([P, len(gates) * N], U8, name="w_plane", align_bytes=64)
         nc.vector.memset(w_plane[:].bitcast(I32), 0)
 
@@ -108,8 +107,6 @@ def tile_list_tgn_gru_kernel(
             page = keep.tile([P, T], F32, name=f"page{len(pages)}", tag=tag, align_bytes=64)
             eng.memset(page[:], 0.0)
             pages.append(page)
-
-        clear_page("page0", nc.vector)
 
         n_cols = n_w + len(gates) * TILES
         turned = psum.tile([P, P], F32, name="keep_n", tag="keep_n")
@@ -195,16 +192,10 @@ def tile_list_tgn_gru_kernel(
             w_pass(xn, "n", t, h, True, True)
             w_pass(sz, "z", t, h, True, False)
             u_pass(sz, "z", t, h, False, True)
-            if s == 1:
-                r = keep.tile([P, JC], F32, name="second_r", align_bytes=64)
-            else:
-                r = work.tile([P, JC], F32, name="r")
+            r = work.tile([P, JC], F32, name="r")
             nc.scalar.activation(r[:], sr[:], ACT.Sigmoid, bias=bias("r", t))
-            if s == 0:
-                xb = xn
-            else:
-                xb = work.tile([P, JC], F32, name="xb")
-                nc.scalar.activation(xb[:], xn[:], ACT.Identity, bias=bias("n", t))
+            xb = work.tile([P, JC], F32, name="xb")
+            nc.scalar.activation(xb[:], xn[:], ACT.Identity, bias=bias("n", t))
             z = work.tile([P, JC], F32, name="z")
             nc.scalar.activation(z[:], sz[:], ACT.Sigmoid, bias=bias("z", t))
             rh = first_rh[s] if s < 2 else mix2[(s - 1) % 2]
@@ -235,22 +226,6 @@ def tile_list_tgn_gru_kernel(
             nc.scalar.copy(fresh_sb[:], fresh_n[:])
             keep_of[s], fresh_of[s] = keep_sb, fresh_sb
 
-        def first_candidate():
-            pre = keep.tile([P, JC], F32, name="first_pre")
-            nc.vector.tensor_tensor(pre[:], xn_of[0][:], rh_of[0][:], ALU.add)
-            cd = keep.tile([P, JC], F32, name="first_cd")
-            nc.scalar.activation(cd[:], pre[:], ACT.Tanh, bias=bias("n", 0))
-            return cd
-
-        def first_place(cd):
-            diff = keep.tile([P, JC], F32, name="first_diff")
-            nc.vector.tensor_tensor(diff[:], state[0][:].indirect(picks(0)), cd[:], ALU.subtract)
-            step = keep.tile([P, JC], F32, name="first_step")
-            nc.vector.scalar_tensor_tensor(step[:], z_of[0][:], 1.0, diff[:], ALU.subtract, ALU.mult)
-            new = keep.tile([P, JC], F32, name="first_new", tag="second_r", align_bytes=64)
-            nc.vector.tensor_tensor(new[:], cd[:], step[:], ALU.subtract)
-            nc.vector.tensor_tensor(pages[0][:].indirect(picks(0)), new[:], first_w[:], ALU.mult)
-
         def look_up(s):
             t, h = steps[s]
             nc.vector.tensor_tensor(mix[s % 2][:], state[t][:].indirect(picks(h)), keep_of[s][:], ALU.mult)
@@ -269,29 +244,24 @@ def tile_list_tgn_gru_kernel(
         x_op[0] = quantise(x_raw[0][:], JC, "x0", nc.scalar.copy, "x0_grouped")
         quantise_u(0)
         gather_table(1, "u_n0_grouped")
+        clear_page("x0_grouped", nc.vector)
         load_x(1, "tab")
         u_tags = {"r": "u_first_r", "n": "u_first_n", "z": "u_r0_grouped"}
         for g in gates:
             load_u(g, 1, 2, u_tags[g])
         load_state(0, "x_raw0")
-        first_w = keep.tile([P, JC], F32, name="first_w", tag="x0_grouped", align_bytes=64)
-        nc.sync.dma_start(first_w[:], wgo[:, 0:JC])
         products(0)
         x_op[1] = quantise(x_raw[1][:], JC, "x1", nc.vector.tensor_copy, "x1_grouped")
         load_state(1, "tab")
-        cd = first_candidate()
-        products(1)
-        quantise_u(1)
-        clear_page("u_z1_grouped", nc.gpsimd)
-        for g in gates:
-            load_u(g, 2, TILES, u_tags[g])
-        first_place(cd)
-        for s in range(1, len(steps)):
-            t, h = steps[s]
+        for s, (t, h) in enumerate(steps):
             factors(s)
             look_up(s)
-            if h == 1 and 1 <= t < TILES - 1:
+            if h == 1 and t + 1 < TILES:
                 quantise_u(t + 1)
+            if s == 1:
+                clear_page("u_z1_grouped", nc.gpsimd)
+                for g in gates:
+                    load_u(g, 2, TILES, u_tags[g])
             if s + 1 < len(steps):
                 products(s + 1)
             place(s)

from contextlib import ExitStack

import concourse.mybir as mybir
from concourse.masks import make_identity

K, M, N, T, J = 512, 512, 512, 2048, 1024
FLOPS = 6 * 2 * K * N * J

F32 = mybir.dt.float32
BF16 = mybir.dt.bfloat16
I32 = mybir.dt.int32
U32 = mybir.dt.uint32
U16 = mybir.dt.uint16
U8 = mybir.dt.uint8
FP8X4 = mybir.dt.float8_e4m3fn_x4
FP4X4 = mybir.dt.float4_e2m1fn_x4
ACT = mybir.ActivationFunctionType
ALU = mybir.AluOpType

P = 128
PACK = 4
JC = 512
HALVES = J // JC
TILES = N // P
BLOCKS = JC // P
LIST_COLS = JC // 16


def tile_list_tgn_gru_kernel(
    tc, x, tab_words, tab_scales, wz_words, wz_scales, uz, wr_words, wr_scales, ur,
    wn_words, wn_scales, un, bz, br, bn, hT, wgo, offs, out,
):
    nc = tc.nc
    gates = ("r", "n", "z")
    w_words = {"r": wr_words, "n": wn_words, "z": wz_words}
    w_scales = {"r": wr_scales, "n": wn_scales, "z": wz_scales}
    u_dram = {"r": ur, "n": un, "z": uz}
    b_dram = {"r": br, "n": bn, "z": bz}

    with ExitStack() as ctx:
        keep = ctx.enter_context(tc.tile_pool(name="keep", bufs=1))
        work = ctx.enter_context(tc.tile_pool(name="work", bufs=2))
        psum = ctx.enter_context(tc.psum_pool(name="psum", bufs=1))

        offsets = keep.tile([P, J // 16], U16, name="offsets")
        nc.sync.dma_start(offsets[:], offs)

        def picks(half):
            return offsets[:, half * LIST_COLS:(half + 1) * LIST_COLS]

        tab_plane = keep.tile([P, T], U8, name="tab_plane", align_bytes=64)
        nc.gpsimd.memset(tab_plane[:].bitcast(I32), 0)
        w_plane = keep.tile([P, len(gates) * N], U8, name="w_plane", align_bytes=64)
        nc.vector.memset(w_plane[:].bitcast(I32), 0)

        rows = keep.tile([P, P], F32, name="rows")
        nc.gpsimd.memset(rows[:], 0.0)
        ident = keep.tile([P, P], F32, name="ident")
        make_identity(nc, ident[:])
        w_rows = keep.tile([16, len(gates) * N], U8, name="w_rows")
        for gi, g in enumerate(gates):
            nc.sync.dma_start(w_rows[:, gi * N:(gi + 1) * N].bitcast(I32), w_scales[g][0].bitcast(I32))
        tab = keep.tile([P, T], I32, name="tab", align_bytes=64)
        for q in range(4):
            nc.sync.dma_start(tab_plane[32 * q:32 * q + 4, :].bitcast(I32),
                              tab_scales[0, 4 * q:4 * q + 4, :].bitcast(I32))
        nc.sync.dma_start(tab[:], tab_words[0].rearrange("p t i -> p (t i)").bitcast(I32))
        n_w = J // P

        for gi, g in enumerate(gates):
            nc.gpsimd.dma_start(rows[n_w + gi * TILES:n_w + (gi + 1) * TILES, :],
                                b_dram[g].rearrange("(t p) -> t p", p=P))
        nc.gpsimd.dma_start(rows[0:n_w, :], wgo[0].rearrange("(c p) -> c p", p=P))

        x_raw = {}

        def load_x(h, tag):
            x_raw[h] = keep.tile([P, PACK, JC], F32, name=f"x_raw{h}", tag=tag, align_bytes=64)
            nc.sync.dma_start(x_raw[h][:], x[:, h * JC:(h + 1) * JC].rearrange("(p i) j -> p i j", i=PACK))

        load_x(0, "x_raw0")
        w_codes = {}
        u_first = {}
        u_rest = {}
        for g in gates:
            w_codes[g] = keep.tile([P, 2 * N], U8, name=f"w_codes_{g}", align_bytes=64)
            u_first[g] = keep.tile([P, PACK, P], F32, name=f"u_first_{g}", align_bytes=64)
            nc.sync.dma_start(u_first[g][:], u_dram[g][:, 0:P].rearrange("(p i) n -> p i n", i=PACK))
            nc.sync.dma_start(w_codes[g][:].bitcast(I32), w_words[g][0].bitcast(I32))
        for q in range(4):
            nc.sync.dma_start(w_plane[32 * q:32 * q + 4, :].bitcast(I32), w_rows[4 * q:4 * q + 4, :].bitcast(I32))
        state = {}

        def load_state(t, tag):
            state[t] = keep.tile([P, T], F32, name=f"state{t}", tag=tag, align_bytes=64)
            nc.sync.dma_start(state[t][:], hT[t * P:(t + 1) * P, :])

        def load_u(g, t0, t1, tag):
            raw = keep.tile([P, PACK, (t1 - t0) * P], F32, name=f"u_raw_{g}{t0}", tag=tag, align_bytes=64)
            nc.sync.dma_start(raw[:], u_dram[g][:, t0 * P:t1 * P].rearrange("(p i) n -> p i n", i=PACK))
            for t in range(t0, t1):
                u_rest[g, t] = raw[:, :, (t - t0) * P:(t - t0 + 1) * P]

        pages = []

        def clear_page(tag, eng):
            page = keep.tile([P, T], F32, name=f"page{len(pages)}", tag=tag, align_bytes=64)
            eng.memset(page[:], 0.0)
            pages.append(page)

        n_cols = n_w + len(gates) * TILES
        turned = psum.tile([P, P], F32, name="keep_n", tag="keep_n")
        nc.tensor.transpose(turned[:], rows[:], ident[:])
        cols = keep.tile([P, n_cols], F32, name="cols")
        nc.scalar.copy(cols[:], turned[:, 0:n_cols])
        minus_w = keep.tile([P, n_w], F32, name="minus_w")
        nc.vector.tensor_scalar(minus_w[:], cols[:, 0:n_w], -1.0, None, ALU.mult)

        def bias(g, t):
            c = n_w + gates.index(g) * TILES + t
            return cols[:, c:c + 1]

        def quantise(raw, width, name, copy, tag):
            grouped = keep.tile([P, width, PACK], BF16, name=f"{name}_grouped", tag=tag, align_bytes=64)
            copy(grouped[:].rearrange("p (c s) i -> p c i s", s=4),
                 raw.rearrange("p i (c s) -> p c i s", s=4))
            codes = keep.tile([P, width], U32, name=f"{name}_codes", align_bytes=64)
            plane = keep.tile([P, width], U8, name=f"{name}_plane", align_bytes=64)
            nc.vector.quantize_mx(out=codes[:].bitcast(FP8X4), scales=plane[:],
                                  in_=grouped[:].rearrange("p w i -> p (w i)"))
            return codes, plane

        v_op = {}
        x_op = {}
        u_op = {}

        def gather_table(h, tag):
            plane = keep.tile([P, JC], U8, name=f"v_plane{h}", tag=tag, align_bytes=64)
            nc.vector.tensor_copy(plane[:], tab_plane[:].indirect(picks(h)))
            codes = keep.tile([P, JC], U32, name=f"v_codes{h}", align_bytes=64)
            nc.vector.tensor_copy(codes[:], tab[:].bitcast(U32).indirect(picks(h)))
            v_op[h] = (codes, plane)

        def quantise_u(t):
            for g in gates:
                raw = u_first[g][:] if t == 0 else u_rest[g, t]
                u_op[g, t] = quantise(raw, P, f"u_{g}{t}", nc.vector.tensor_copy if t == 0 else nc.scalar.copy,
                                      f"u_{g}{t}_grouped")

        def w_pass(acc, g, t, h, start, stop):
            gi = gates.index(g)
            nc.tensor.matmul_mx(
                out=acc[:], lhsT=w_codes[g][:, 2 * P * t:2 * P * (t + 1)].bitcast(FP4X4),
                lhsT_scale=w_plane[:, gi * N + t * P:gi * N + (t + 1) * P],
                rhs=x_op[h][0][:].bitcast(FP8X4), rhs_scale=x_op[h][1][:], start=start, stop=stop)

        def u_pass(acc, g, t, h, start, stop):
            nc.tensor.matmul_mx(
                out=acc[:], lhsT=u_op[g, t][0][:].bitcast(FP8X4), lhsT_scale=u_op[g, t][1][:],
                rhs=v_op[h][0][:].bitcast(FP8X4), rhs_scale=v_op[h][1][:], start=start, stop=stop)

        def block(b):
            return slice(b * P, (b + 1) * P)

        def turn(name, *terms):
            bank = psum.tile([P, JC], F32, name=name, tag=name)
            for b in range(BLOCKS):
                for i, term in enumerate(terms):
                    nc.tensor.matmul(bank[:, block(b)], lhsT=term[:, block(b)], rhs=ident[:], is_transpose=True,
                                     start=(i == 0), stop=(i == len(terms) - 1))
            return bank

        steps = [(t, h) for t in range(TILES) for h in range(HALVES)]
        mix = [keep.tile([P, JC], F32, name=f"mix{b}") for b in range(2)]
        mix2 = [keep.tile([P, JC], F32, name=f"mixb{b}") for b in range(2)]
        first_rh = [keep.tile([P, JC], F32, name=f"first_rh{b}") for b in range(2)]
        z_of = {}
        xn_of = {}
        rh_of = {}
        keep_of = {}
        fresh_of = {}

        def products(s):
            t, h = steps[s]
            sr = psum.tile([P, JC], F32, name="sr")
            hn = psum.tile([P, JC], F32, name="hn")
            xn = psum.tile([P, JC], F32, name="xn")
            sz = psum.tile([P, JC], F32, name="sz")
            w_pass(sr, "r", t, h, True, False)
            u_pass(sr, "r", t, h, False, True)
            u_pass(hn, "n", t, h, True, True)
            w_pass(xn, "n", t, h, True, True)
            w_pass(sz, "z", t, h, True, False)
            u_pass(sz, "z", t, h, False, True)
            r = work.tile([P, JC], F32, name="r")
            nc.scalar.activation(r[:], sr[:], ACT.Sigmoid, bias=bias("r", t))
            xb = work.tile([P, JC], F32, name="xb")
            nc.scalar.activation(xb[:], xn[:], ACT.Identity, bias=bias("n", t))
            z = work.tile([P, JC], F32, name="z")
            nc.scalar.activation(z[:], sz[:], ACT.Sigmoid, bias=bias("z", t))
            rh = first_rh[s] if s < 2 else mix2[(s - 1) % 2]
            nc.vector.tensor_tensor(rh[:], hn[:], r[:], ALU.mult)
            z_of[s], xn_of[s], rh_of[s] = z, xb, rh

        def factors(s):
            t, h = steps[s]
            pre_t = turn("pre_t", xn_of[s], rh_of[s])
            z_t = turn("z_t", z_of[s])
            minus_cd_t = mix[s % 2]
            nc.scalar.activation(minus_cd_t[:], pre_t[:], ACT.Tanh, scale=-1.0)
            keep_t = work.tile([P, JC], F32, name="keep_t")
            for b in range(BLOCKS):
                c = h * BLOCKS + b
                nc.scalar.activation(keep_t[:, block(b)], z_t[:, block(b)], ACT.Identity,
                                     scale=minus_w[:, c:c + 1], bias=cols[:, c:c + 1])
            keep_n = turn("keep_n", keep_t)
            keep_sb = mix2[s % 2]
            nc.scalar.copy(keep_sb[:], keep_n[:])
            fresh_t = work.tile([P, JC], F32, name="fresh_t")
            for b in range(BLOCKS):
                c = h * BLOCKS + b
                nc.vector.scalar_tensor_tensor(fresh_t[:, block(b)], keep_t[:, block(b)], cols[:, c:c + 1],
                                               minus_cd_t[:, block(b)], ALU.subtract, ALU.mult)
            fresh_n = turn("fresh_n", fresh_t)
            fresh_sb = work.tile([P, JC], F32, name="fresh_sb", bufs=3)
            nc.scalar.copy(fresh_sb[:], fresh_n[:])
            keep_of[s], fresh_of[s] = keep_sb, fresh_sb

        def look_up(s):
            t, h = steps[s]
            nc.vector.tensor_tensor(mix[s % 2][:], state[t][:].indirect(picks(h)), keep_of[s][:], ALU.mult)

        def place(s):
            t, h = steps[s]
            kept = mix[s % 2]
            page = pages[t % 2]
            nc.vector.tensor_tensor(page[:].indirect(picks(h)), kept[:], fresh_of[s][:], ALU.add)
            if h == HALVES - 1:
                if t + 2 < TILES:
                    load_state(t + 2, "x_raw0" if t % 2 == 0 else "tab")
                nc.sync.dma_start(out[t * P:(t + 1) * P, :], page[:])

        gather_table(0, "v_plane0")
        x_op[0] = quantise(x_raw[0][:], JC, "x0", nc.scalar.copy, "x0_grouped")
        quantise_u(0)
        gather_table(1, "u_n0_grouped")
        clear_page("x0_grouped", nc.vector)
        load_x(1, "tab")
        u_tags = {"r": "u_first_r", "n": "u_first_n", "z": "u_r0_grouped"}
        for g in gates:
            load_u(g, 1, 2, u_tags[g])
        load_state(0, "x_raw0")
        products(0)
        x_op[1] = quantise(x_raw[1][:], JC, "x1", nc.vector.tensor_copy, "x1_grouped")
        load_state(1, "tab")
        for s, (t, h) in enumerate(steps):
            factors(s)
            look_up(s)
            if h == 1 and t + 1 < TILES:
                quantise_u(t + 1)
            if s == 1:
                clear_page("u_z1_grouped", nc.gpsimd)
                for g in gates:
                    load_u(g, 2, TILES, u_tags[g])
            if s + 1 < len(steps):
                products(s + 1)
            place(s)
